import numpy as np
import ml_dtypes


def mxq(x, axis, fmt="e4m3"):
    dtype, down = {"e4m3": (ml_dtypes.float8_e4m3fn, 7), "e5m2": (ml_dtypes.float8_e5m2, 14)}[fmt]
    v = np.moveaxis(np.asarray(x, np.float32).astype(ml_dtypes.bfloat16).astype(np.float64), axis, -1)
    blocks = v.reshape(v.shape[:-1] + (-1, 32))
    amax = np.abs(blocks).max(-1, keepdims=True)
    byte = np.maximum(np.where(amax > 0, np.frexp(amax)[1] - 1 + 127, 0) - down, 1)
    scale = np.exp2(byte - 127.0)
    codes = (blocks / scale).astype(np.float32).astype(dtype).astype(np.float64)
    return np.moveaxis((codes * scale).reshape(v.shape), -1, axis)


WIDE = False


def mx_kscale(k):
    if not WIDE:
        return np.ones(k)
    levels = np.array([10, -10, 5, -5, 0])
    if k % 512:
        return np.exp2(np.random.permutation(np.resize(levels, k // 32))).repeat(32)
    a = np.empty((k // 512, 16))
    for p in range(k // 512):
        a[p, :8] = np.random.permutation(np.resize(levels, 8))
        for g in range(8):
            far = levels[np.abs(levels - a[p, g]) >= 10]
            a[p, g + 8] = far[np.random.randint(len(far))]
    return np.exp2(a.ravel()).repeat(32)


def f64(x):
    return np.asarray(x).astype(np.float64)


def striped(idx):
    return np.tile(idx.reshape(-1, 16).T, (8, 1)).astype(np.uint16)


def unstriped(offs):
    return offs[:16].T.reshape(-1).astype(np.int64)


def pack_weight(w):
    k, n = w.shape
    w = f64(np.asarray(w, np.float32).astype(ml_dtypes.bfloat16)).reshape(k // 32, 32, n)
    amax = np.abs(w).max(1)
    byte = np.clip(np.where(amax > 0, np.frexp(amax)[1] - 1 + 127 - 7, 1), 1, 254)
    scaled = (w * np.exp2(127.0 - byte)[:, None, :]).reshape(k, n).astype(np.float32)
    words = np.ascontiguousarray(scaled.reshape(k // 512, 128, 4, n).transpose(0, 1, 3, 2)).astype(ml_dtypes.float8_e4m3fn).view(np.uint8)
    return words, np.ascontiguousarray(byte.astype(np.uint8).reshape(k // 512, 16, n))


def unpack_weight(words, scales):
    g, p, n, _ = words.shape
    vals = np.ascontiguousarray(words).view(ml_dtypes.float8_e4m3fn).astype(np.float64) * np.repeat(np.exp2(scales.astype(np.float64) - 127.0), 8, axis=1)[..., None]
    return vals.transpose(0, 1, 3, 2).reshape(g * 512, n)


def planes(y):
    n, m = y.shape
    v = y.astype(np.float32).astype(ml_dtypes.bfloat16).astype(np.float64).reshape(n // 32, 32, m)
    top = np.abs(v).max(1)
    byte = np.clip(np.where(top > 0, np.frexp(top)[1] - 1 + 127 - 7, 1), 1, 254)
    codes = (v * np.exp2(127.0 - byte)[:, None, :]).reshape(n, m).astype(np.float32).astype(ml_dtypes.float8_e4m3fn).view(np.uint8)
    words = codes.reshape(n // 512, 128, 4, m).transpose(0, 1, 3, 2)
    return np.ascontiguousarray(words), np.ascontiguousarray(byte.astype(np.uint8).reshape(n // 512, 16, m))


def gelu(v):
    return 0.5 * v * (1.0 + np.tanh(np.sqrt(2.0 / np.pi) * (v + 0.044715 * v**3)))


K, T, S, W, H, N = 512, 1024, 512, 1024, 512, 512


def setup_inputs():
    n = np.random.standard_normal
    s = mx_kscale(K)[:, None]
    u = mx_kscale(H)
    packed_xT = pack_weight(n((K, T)) * s)
    packed_eT = pack_weight(n((K, W)) * s)
    return {
        "x_words": packed_xT[0],
        "x_scales": packed_xT[1],
        "e_words": packed_eT[0],
        "e_scales": packed_eT[1],
        "w1": (n((K, H)) / np.sqrt(2 * K) / s * u).astype(np.float32),
        "w2": (n((K, H)) / np.sqrt(2 * K) / s * u).astype(np.float32),
        "w3": (n((H, N)) / np.sqrt(H) / u[:, None]).astype(np.float32),
        "skip": (n((N, S))).astype(np.float32),
        "offs": striped(np.random.permutation(T)[:S]),
        "tok": striped(np.random.permutation(W)[:S]),
    }


def reference(x_words, x_scales, e_words, e_scales, w1, w2, w3, skip, offs, tok):
    xq = unpack_weight(x_words, x_scales)[:, unstriped(offs)]
    e_tok = unpack_weight(e_words, e_scales)[:, unstriped(tok)]
    h = gelu(mxq(f64(w1), 0, "e4m3").T @ xq + mxq(f64(w2), 0, "e4m3").T @ e_tok)
    y = mxq(f64(w3), 0, "e4m3").T @ mxq(h, 0, "e4m3")
    out_0 = y + f64(skip)
    return (out_0,) + planes(out_0)

@@ -1,0 +1,162 @@
+from contextlib import ExitStack
+
+import concourse.mybir as mybir
+
+F32 = mybir.dt.float32
+BF16 = mybir.dt.bfloat16
+I32 = mybir.dt.int32
+U32 = mybir.dt.uint32
+U16 = mybir.dt.uint16
+U8 = mybir.dt.uint8
+FP8X4 = mybir.dt.float8_e4m3fn_x4
+GELU = mybir.ActivationFunctionType.Gelu_apprx_tanh
+ADD = mybir.AluOpType.add
+
+P = 128
+PACK = 4
+WIDTH = 512
+TABLE = 1024
+BLOCK = 128
+BLOCKS = WIDTH // BLOCK
+HALF = WIDTH // 2
+PER_COLUMN = 16
+
+FLOPS = 3 * 2 * WIDTH * WIDTH * WIDTH
+
+
+def tile_picked_zeagle_gelu_po_kernel(
+    tc, x_words, x_scales, e_words, e_scales, w1, w2, w3, skip, offs, tok, out_0, out_1, out_2
+):
+    nc = tc.nc
+    with ExitStack() as ctx:
+        keep = ctx.enter_context(tc.tile_pool(name="keep", bufs=1))
+        psum = ctx.enter_context(tc.psum_pool(name="psum", bufs=1))
+
+        def sbuf(shape, dtype, name):
+            return keep.tile(shape, dtype, name=name, align_bytes=64)
+
+        offs_sb = keep.tile([P, WIDTH // PER_COLUMN], U16, name="offs_sb")
+        tok_sb = keep.tile([P, WIDTH // PER_COLUMN], U16, name="tok_sb")
+        x_table = sbuf([P, TABLE], U32, "x_table")
+        e_table = sbuf([P, TABLE], U32, "e_table")
+        x_scale_table = sbuf([P, TABLE], U8, "x_scale_table")
+        e_scale_table = sbuf([P, TABLE], U8, "e_scale_table")
+
+        def load_words(table, words):
+            nc.sync.dma_start(table[:].bitcast(I32), words[0].rearrange("p n t -> p (n t)").bitcast(I32))
+
+        def load_scales(queue, table, scales):
+            for q in range(4):
+                queue.dma_start(table[32 * q : 32 * q + 4, :].bitcast(I32), scales[0, 4 * q : 4 * q + 4, :].bitcast(I32))
+
+        def load_halves(matrix, name):
+            halves = []
+            for u in range(2):
+                half = sbuf([P, PACK, HALF], F32, "%s_%d" % (name, u))
+                nc.sync.dma_start(half[:], matrix[:, u * HALF : (u + 1) * HALF].rearrange("(p j) c -> p j c", j=PACK))
+                halves.append(half)
+            return halves
+
+        nc.vector.memset(x_scale_table[:].bitcast(I32), 0)
+        nc.gpsimd.memset(e_scale_table[:].bitcast(I32), 0)
+        nc.sync.dma_start(offs_sb[:], offs)
+        load_words(x_table, x_words)
+        nc.sync.dma_start(tok_sb[:], tok)
+        load_scales(nc.scalar, x_scale_table, x_scales)
+        load_scales(nc.gpsimd, e_scale_table, e_scales)
+        w1_raw = load_halves(w1, "w1_raw")
+        w2_raw = load_halves(w2, "w2_raw")
+        load_words(e_table, e_words)
+        w3_raw = load_halves(w3, "w3_raw")
+        skip_sb = load_halves(skip, "skip_sb")
+
+        def deal(copy, dealt, raw, u):
+            m = slice(u * P // 2, (u + 1) * P // 2)
+            copy(dealt[:, :, m, :].rearrange("p t m j -> p m j t"), raw[u][:].rearrange("p j (m t) -> p m j t", t=PACK))
+
+        def quantise(codes, scales, values):
+            nc.vector.quantize_mx(codes.bitcast(FP8X4), scales, values)
+
+        def mx_tiles(name):
+            return sbuf([P, WIDTH], U32, name + "_codes"), sbuf([P, WIDTH], U8, name + "_scales")
+
+        x_codes, x_sc = mx_tiles("x")
+        e_codes, e_sc = mx_tiles("e")
+        w1_codes, w1_sc = mx_tiles("w1")
+        w2_codes, w2_sc = mx_tiles("w2")
+        w3_codes, w3_sc = mx_tiles("w3")
+        h_codes, h_sc = mx_tiles("h")
+        y_codes, y_sc = mx_tiles("y")
+        w1_dealt = sbuf([P, PACK, P, PACK], BF16, "w1_dealt")
+        w2_dealt = sbuf([P, PACK, P, PACK], BF16, "w2_dealt")
+        w3_dealt = sbuf([P, PACK, P, PACK], BF16, "w3_dealt")
+
+        nc.vector.tensor_copy(x_codes[:], x_table[:].indirect(offs_sb[:]))
+        nc.vector.tensor_copy(x_sc[:], x_scale_table[:].indirect(offs_sb[:]))
+        nc.vector.tensor_copy(e_sc[:], e_scale_table[:].indirect(tok_sb[:]))
+        deal(nc.scalar.copy, w1_dealt, w1_raw, 0)
+        deal(nc.scalar.copy, w1_dealt, w1_raw, 1)
+        quantise(w1_codes[:], w1_sc[:], w1_dealt[:].rearrange("p t m j -> p (t m j)"))
+        deal(nc.scalar.copy, w2_dealt, w2_raw, 0)
+        deal(nc.vector.tensor_copy, w2_dealt, w2_raw, 1)
+        quantise(w2_codes[:], w2_sc[:], w2_dealt[:].rearrange("p t m j -> p (t m j)"))
+
+        def cols(b):
+            return slice(b * BLOCK, (b + 1) * BLOCK)
+
+        def product(acc, w_codes, w_sc, t, codes, sc, b, start, stop):
+            nc.tensor.matmul_mx(
+                acc[:, t, :],
+                lhsT=w_codes[:, cols(t)].bitcast(FP8X4),
+                lhsT_scale=w_sc[:, cols(t)],
+                rhs=codes[:, cols(b)].bitcast(FP8X4),
+                rhs_scale=sc[:, cols(b)],
+                start=start,
+                stop=stop,
+            )
+
+        h_values = []
+        for b in range(BLOCKS):
+            entries = slice(b * BLOCK // PER_COLUMN, (b + 1) * BLOCK // PER_COLUMN)
+            nc.vector.tensor_copy(e_codes[:, cols(b)], e_table[:].indirect(tok_sb[:, entries]))
+            acc = psum.tile([P, PACK, BLOCK], F32, name="h_acc_%d" % b)
+            for t in range(PACK):
+                product(acc, w1_codes, w1_sc, t, x_codes, x_sc, b, True, False)
+                product(acc, w2_codes, w2_sc, t, e_codes, e_sc, b, False, True)
+            h = sbuf([P, BLOCK, PACK], BF16, "h_%d" % b)
+            nc.scalar.activation(h[:], acc[:].rearrange("p t n -> p n t"), GELU)
+            h_values.append(h)
+            if b == 0:
+                deal(nc.scalar.copy, w3_dealt, w3_raw, 0)
+
+        deal(nc.vector.tensor_copy, w3_dealt, w3_raw, 1)
+        quantise(h_codes[:, cols(0)], h_sc[:, cols(0)], h_values[0][:].rearrange("p n t -> p (n t)"))
+        quantise(w3_codes[:], w3_sc[:], w3_dealt[:].rearrange("p t m j -> p (t m j)"))
+        for b in range(1, BLOCKS):
+            quantise(h_codes[:, cols(b)], h_sc[:, cols(b)], h_values[b][:].rearrange("p n t -> p (n t)"))
+
+        out_rows = out_0.rearrange("(p t) n -> p t n", t=PACK)
+        out_words = out_1[0].rearrange("p n t -> p (n t)").bitcast(I32)
+        rounded = []
+        for b in range(BLOCKS):
+            acc = psum.tile([P, PACK, BLOCK], F32, name="y_acc_%d" % b)
+            for t in range(PACK):
+                product(acc, w3_codes, w3_sc, t, h_codes, h_sc, b, True, True)
+            y = sbuf([P, PACK, BLOCK], F32, "y_%d" % b)
+            nc.vector.tensor_tensor(y[:], acc[:], skip_sb[b // 2][:, :, cols(b % 2)], ADD)
+            nc.sync.dma_start(out_rows[:, :, cols(b)], y[:])
+            y16 = sbuf([P, BLOCK, PACK], BF16, "y16_%d" % b)
+            nc.scalar.copy(
+                y16[:].rearrange("p (c i) t -> p c t i", i=PACK), y[:].rearrange("p t (c i) -> p c t i", i=PACK)
+            )
+            rounded.append(y16)
+            if b > 0:
+                quantise(y_codes[:, cols(b - 1)], y_sc[:, cols(b - 1)], rounded[b - 1][:].rearrange("p n t -> p (n t)"))
+            if b == 2:
+                nc.sync.dma_start(out_words[:, 0:HALF], y_codes[:, 0:HALF].bitcast(I32))
+        last = BLOCKS - 1
+        quantise(y_codes[:, cols(last)], y_sc[:, cols(last)], rounded[last][:].rearrange("p n t -> p (n t)"))
+        nc.sync.dma_start(out_words[:, HALF:WIDTH], y_codes[:, HALF:WIDTH].bitcast(I32))
+        for q in range(4):
+            queue = nc.scalar if q % 2 == 0 else nc.sync
+            queue.dma_start(out_2[0, 4 * q : 4 * q + 4, :].bitcast(I32), y_sc[32 * q : 32 * q + 4, :].bitcast(I32))

@@ -57,22 +57,40 @@ def tile_picked_zeagle_gelu_po_kernel(
                 halves.append(half)
             return halves
 
-        nc.vector.memset(x_scale_table[:].bitcast(I32), 0)
+        def load_whole(matrix, name):
+            whole = sbuf([P, PACK, WIDTH], F32, name)
+            nc.sync.dma_start(whole[:], matrix.rearrange("(p j) c -> p j c", j=PACK))
+            return whole
+
+        warm_in = sbuf([P, 1], F32, "warm_in")
+        warm_out = sbuf([P, 1], F32, "warm_out")
+        nc.gpsimd.memset(x_scale_table[:].bitcast(I32), 0)
         nc.gpsimd.memset(e_scale_table[:].bitcast(I32), 0)
-        nc.sync.dma_start(offs_sb[:], offs)
+        nc.vector.memset(warm_in[:], 0.0)
+        nc.scalar.activation(warm_out[:], warm_in[:], GELU)
         load_words(x_table, x_words)
+        nc.sync.dma_start(offs_sb[:], offs)
+        load_scales(nc.sync, x_scale_table, x_scales)
+        w1_raw = load_whole(w1, "w1_raw")
         nc.sync.dma_start(tok_sb[:], tok)
-        load_scales(nc.scalar, x_scale_table, x_scales)
-        load_scales(nc.gpsimd, e_scale_table, e_scales)
-        w1_raw = load_halves(w1, "w1_raw")
-        w2_raw = load_halves(w2, "w2_raw")
+        load_scales(nc.sync, e_scale_table, e_scales)
+        w2_raw = load_whole(w2, "w2_raw")
         load_words(e_table, e_words)
-        w3_raw = load_halves(w3, "w3_raw")
+        w3_raw = load_whole(w3, "w3_raw")
         skip_sb = load_halves(skip, "skip_sb")
 
-        def deal(copy, dealt, raw, u):
-            m = slice(u * P // 2, (u + 1) * P // 2)
-            copy(dealt[:, :, m, :].rearrange("p t m j -> p m j t"), raw[u][:].rearrange("p j (m t) -> p m j t", t=PACK))
+        def deal(dealt, raw, on_vector):
+            source = raw[:].rearrange("p j (m t) -> p m j t", t=PACK)
+            target = dealt[:].rearrange("p t m j -> p m j t")
+            nc.scalar.copy(target[:, on_vector:P], source[:, on_vector:P])
+            nc.vector.tensor_copy(target[:, 0:on_vector], source[:, 0:on_vector])
+
+        def cols(b):
+            return slice(b * BLOCK, (b + 1) * BLOCK)
+
+        def quantise_slices(codes, scales, dealt):
+            for t in range(PACK):
+                quantise(codes[:, cols(t)], scales[:, cols(t)], dealt[:, t].rearrange("p m j -> p (m j)"))
 
         def quantise(codes, scales, values):
             nc.vector.quantize_mx(codes.bitcast(FP8X4), scales, values)
@@ -94,15 +112,9 @@ def tile_picked_zeagle_gelu_po_kernel(
         nc.vector.tensor_copy(x_codes[:], x_table[:].indirect(offs_sb[:]))
         nc.vector.tensor_copy(x_sc[:], x_scale_table[:].indirect(offs_sb[:]))
         nc.vector.tensor_copy(e_sc[:], e_scale_table[:].indirect(tok_sb[:]))
-        deal(nc.scalar.copy, w1_dealt, w1_raw, 0)
-        deal(nc.scalar.copy, w1_dealt, w1_raw, 1)
+        deal(w1_dealt, w1_raw, 48)
         quantise(w1_codes[:], w1_sc[:], w1_dealt[:].rearrange("p t m j -> p (t m j)"))
-        deal(nc.scalar.copy, w2_dealt, w2_raw, 0)
-        deal(nc.vector.tensor_copy, w2_dealt, w2_raw, 1)
-        quantise(w2_codes[:], w2_sc[:], w2_dealt[:].rearrange("p t m j -> p (t m j)"))
-
-        def cols(b):
-            return slice(b * BLOCK, (b + 1) * BLOCK)
+        deal(w2_dealt, w2_raw, 88)
 
         def product(acc, w_codes, w_sc, t, codes, sc, b, start, stop):
             nc.tensor.matmul_mx(
@@ -119,6 +131,8 @@ def tile_picked_zeagle_gelu_po_kernel(
         for b in range(BLOCKS):
             entries = slice(b * BLOCK // PER_COLUMN, (b + 1) * BLOCK // PER_COLUMN)
             nc.vector.tensor_copy(e_codes[:, cols(b)], e_table[:].indirect(tok_sb[:, entries]))
+            if b == 0:
+                quantise_slices(w2_codes, w2_sc, w2_dealt)
             acc = psum.tile([P, PACK, BLOCK], F32, name="h_acc_%d" % b)
             for t in range(PACK):
                 product(acc, w1_codes, w1_sc, t, x_codes, x_sc, b, True, False)
@@ -126,12 +140,11 @@ def tile_picked_zeagle_gelu_po_kernel(
             h = sbuf([P, BLOCK, PACK], BF16, "h_%d" % b)
             nc.scalar.activation(h[:], acc[:].rearrange("p t n -> p n t"), GELU)
             h_values.append(h)
-            if b == 0:
-                deal(nc.scalar.copy, w3_dealt, w3_raw, 0)
+            if b == 1:
+                deal(w3_dealt, w3_raw, 88)
 
-        deal(nc.vector.tensor_copy, w3_dealt, w3_raw, 1)
         quantise(h_codes[:, cols(0)], h_sc[:, cols(0)], h_values[0][:].rearrange("p n t -> p (n t)"))
-        quantise(w3_codes[:], w3_sc[:], w3_dealt[:].rearrange("p t m j -> p (t m j)"))
+        quantise_slices(w3_codes, w3_sc, w3_dealt)
         for b in range(1, BLOCKS):
             quantise(h_codes[:, cols(b)], h_sc[:, cols(b)], h_values[b][:].rearrange("p n t -> p (n t)"))
 
@@ -152,11 +165,10 @@ def tile_picked_zeagle_gelu_po_kernel(
             rounded.append(y16)
             if b > 0:
                 quantise(y_codes[:, cols(b - 1)], y_sc[:, cols(b - 1)], rounded[b - 1][:].rearrange("p n t -> p (n t)"))
-            if b == 2:
-                nc.sync.dma_start(out_words[:, 0:HALF], y_codes[:, 0:HALF].bitcast(I32))
         last = BLOCKS - 1
+        nc.sync.dma_start(out_words[:, 0 : last * BLOCK], y_codes[:, 0 : last * BLOCK].bitcast(I32))
         quantise(y_codes[:, cols(last)], y_sc[:, cols(last)], rounded[last][:].rearrange("p n t -> p (n t)"))
-        nc.sync.dma_start(out_words[:, HALF:WIDTH], y_codes[:, HALF:WIDTH].bitcast(I32))
+        nc.sync.dma_start(out_words[:, cols(last)], y_codes[:, cols(last)].bitcast(I32))
         for q in range(4):
             queue = nc.scalar if q % 2 == 0 else nc.sync
             queue.dma_start(out_2[0, 4 * q : 4 * q + 4, :].bitcast(I32), y_sc[32 * q : 32 * q + 4, :].bitcast(I32))

@@ -14,12 +14,20 @@ ADD = mybir.AluOpType.add
 
 P = 128
 PACK = 4
+QUADRANT = 32
+SCALE_ROWS = 16
 WIDTH = 512
 TABLE = 1024
 BLOCK = 128
 BLOCKS = WIDTH // BLOCK
 HALF = WIDTH // 2
 PER_COLUMN = 16
+
+E_SCALE_START = 4
+W1_ON_VECTOR = 32
+W2_ON_VECTOR = 80
+LAST_ON_SCALAR = BLOCK // PACK // 2
+WARM_UP_PASSES = 2
 
 FLOPS = 3 * 2 * WIDTH * WIDTH * WIDTH
 
@@ -32,8 +40,55 @@ def tile_picked_zeagle_gelu_po_kernel(
         keep = ctx.enter_context(tc.tile_pool(name="keep", bufs=1))
         psum = ctx.enter_context(tc.psum_pool(name="psum", bufs=1))
 
-        def sbuf(shape, dtype, name):
-            return keep.tile(shape, dtype, name=name, align_bytes=64)
+        def sbuf(shape, dtype, name, tag=None):
+            return keep.tile(shape, dtype, name=name, tag=tag or name, align_bytes=64)
+
+        def cols(b):
+            return slice(b * BLOCK, (b + 1) * BLOCK)
+
+        def load_words(table, words):
+            nc.sync.dma_start(table[:].bitcast(I32), words[0].rearrange("p n t -> p (n t)").bitcast(I32))
+
+        def load_scales(table, scales, start):
+            for r in range(PACK):
+                nc.sync.dma_start(
+                    table[start + r : P : QUADRANT, :].bitcast(I32), scales[0, r:SCALE_ROWS:PACK, :].bitcast(I32)
+                )
+
+        def load_rows(matrix, name):
+            rows = sbuf([P, PACK, matrix.shape[1]], F32, name)
+            nc.sync.dma_start(rows[:], matrix.rearrange("(p j) c -> p j c", j=PACK))
+            return rows
+
+        def deal(copy, dealt, raw, groups):
+            source = raw[:].rearrange("p j (m t) -> p m j t", t=PACK)
+            target = dealt[:].rearrange("p t m j -> p m j t")
+            copy(target[:, groups], source[:, groups])
+
+        def deal_shared(dealt, raw, on_vector):
+            deal(nc.scalar.copy, dealt, raw, slice(on_vector, P))
+            deal(nc.vector.tensor_copy, dealt, raw, slice(0, on_vector))
+
+        def quantise(codes, scales, values):
+            nc.vector.quantize_mx(codes.bitcast(FP8X4), scales, values)
+
+        def quantise_slices(codes, scales, dealt):
+            for t in range(PACK):
+                quantise(codes[:, cols(t)], scales[:, cols(t)], dealt[:, t].rearrange("p m j -> p (m j)"))
+
+        def quantise_block(codes, scales, values, b):
+            quantise(codes[:, cols(b)], scales[:, cols(b)], values[:].rearrange("p n t -> p (n t)"))
+
+        def product(acc, w_codes, w_scales, t, codes, scales, start, stop):
+            nc.tensor.matmul_mx(
+                acc,
+                lhsT=w_codes[:, cols(t)].bitcast(FP8X4),
+                lhsT_scale=w_scales[:, cols(t)],
+                rhs=codes.bitcast(FP8X4),
+                rhs_scale=scales,
+                start=start,
+                stop=stop,
+            )
 
         offs_sb = keep.tile([P, WIDTH // PER_COLUMN], U16, name="offs_sb")
         tok_sb = keep.tile([P, WIDTH // PER_COLUMN], U16, name="tok_sb")
@@ -42,69 +97,31 @@ def tile_picked_zeagle_gelu_po_kernel(
         x_scale_table = sbuf([P, TABLE], U8, "x_scale_table")
         e_scale_table = sbuf([P, TABLE], U8, "e_scale_table")
 
-        def load_words(table, words):
-            nc.sync.dma_start(table[:].bitcast(I32), words[0].rearrange("p n t -> p (n t)").bitcast(I32))
-
-        def load_scales(queue, table, scales):
-            for q in range(4):
-                queue.dma_start(table[32 * q : 32 * q + 4, :].bitcast(I32), scales[0, 4 * q : 4 * q + 4, :].bitcast(I32))
-
-        def load_halves(matrix, name):
-            halves = []
-            for u in range(2):
-                half = sbuf([P, PACK, HALF], F32, "%s_%d" % (name, u))
-                nc.sync.dma_start(half[:], matrix[:, u * HALF : (u + 1) * HALF].rearrange("(p j) c -> p j c", j=PACK))
-                halves.append(half)
-            return halves
-
-        def load_whole(matrix, name):
-            whole = sbuf([P, PACK, WIDTH], F32, name)
-            nc.sync.dma_start(whole[:], matrix.rearrange("(p j) c -> p j c", j=PACK))
-            return whole
-
         warm_in = sbuf([P, 1], F32, "warm_in")
         warm_out = sbuf([P, 1], F32, "warm_out")
-        nc.gpsimd.memset(x_scale_table[:].bitcast(I32), 0)
+        nc.vector.memset(x_scale_table[:].bitcast(I32), 0)
         nc.gpsimd.memset(e_scale_table[:].bitcast(I32), 0)
         nc.vector.memset(warm_in[:], 0.0)
         nc.scalar.activation(warm_out[:], warm_in[:], GELU)
+
         load_words(x_table, x_words)
         nc.sync.dma_start(offs_sb[:], offs)
-        load_scales(nc.sync, x_scale_table, x_scales)
-        w1_raw = load_whole(w1, "w1_raw")
         nc.sync.dma_start(tok_sb[:], tok)
-        load_scales(nc.sync, e_scale_table, e_scales)
-        w2_raw = load_whole(w2, "w2_raw")
+        load_scales(x_scale_table, x_scales, 0)
+        w1_raw = load_rows(w1, "w1_raw")
+        load_scales(e_scale_table, e_scales, E_SCALE_START)
+        w2_raw = load_rows(w2, "w2_raw")
         load_words(e_table, e_words)
-        w3_raw = load_whole(w3, "w3_raw")
-        skip_sb = load_halves(skip, "skip_sb")
+        w3_raw = load_rows(w3, "w3_raw")
+        skip_sb = [load_rows(skip[:, u * HALF : (u + 1) * HALF], "skip_%d" % u) for u in range(2)]
 
-        def deal(dealt, raw, on_vector):
-            source = raw[:].rearrange("p j (m t) -> p m j t", t=PACK)
-            target = dealt[:].rearrange("p t m j -> p m j t")
-            nc.scalar.copy(target[:, on_vector:P], source[:, on_vector:P])
-            nc.vector.tensor_copy(target[:, 0:on_vector], source[:, 0:on_vector])
-
-        def cols(b):
-            return slice(b * BLOCK, (b + 1) * BLOCK)
-
-        def quantise_slices(codes, scales, dealt):
-            for t in range(PACK):
-                quantise(codes[:, cols(t)], scales[:, cols(t)], dealt[:, t].rearrange("p m j -> p (m j)"))
-
-        def quantise(codes, scales, values):
-            nc.vector.quantize_mx(codes.bitcast(FP8X4), scales, values)
-
-        def mx_tiles(name):
-            return sbuf([P, WIDTH], U32, name + "_codes"), sbuf([P, WIDTH], U8, name + "_scales")
-
-        x_codes, x_sc = mx_tiles("x")
-        e_codes, e_sc = mx_tiles("e")
-        w1_codes, w1_sc = mx_tiles("w1")
-        w2_codes, w2_sc = mx_tiles("w2")
-        w3_codes, w3_sc = mx_tiles("w3")
-        h_codes, h_sc = mx_tiles("h")
-        y_codes, y_sc = mx_tiles("y")
+        x_codes, x_sc = sbuf([P, WIDTH], U32, "x_codes"), sbuf([P, WIDTH], U8, "x_sc")
+        e_codes, e_sc = sbuf([P, WIDTH], U32, "e_codes"), sbuf([P, WIDTH], U8, "e_sc")
+        w1_codes = sbuf([P, WIDTH], U32, "w1_codes")
+        w2_codes, w2_sc = sbuf([P, WIDTH], U32, "w2_codes"), sbuf([P, WIDTH], U8, "w2_sc")
+        w3_codes, w3_sc = sbuf([P, WIDTH], U32, "w3_codes"), sbuf([P, WIDTH], U8, "w3_sc")
+        h_sc = sbuf([P, WIDTH], U8, "h_sc")
+        y_codes, y_sc = sbuf([P, WIDTH], U32, "y_codes"), sbuf([P, WIDTH], U8, "y_sc")
         w1_dealt = sbuf([P, PACK, P, PACK], BF16, "w1_dealt")
         w2_dealt = sbuf([P, PACK, P, PACK], BF16, "w2_dealt")
         w3_dealt = sbuf([P, PACK, P, PACK], BF16, "w3_dealt")
@@ -112,20 +129,17 @@ def tile_picked_zeagle_gelu_po_kernel(
         nc.vector.tensor_copy(x_codes[:], x_table[:].indirect(offs_sb[:]))
         nc.vector.tensor_copy(x_sc[:], x_scale_table[:].indirect(offs_sb[:]))
         nc.vector.tensor_copy(e_sc[:], e_scale_table[:].indirect(tok_sb[:]))
-        deal(w1_dealt, w1_raw, 48)
+        deal_shared(w1_dealt, w1_raw, W1_ON_VECTOR)
+        w1_sc = sbuf([P, WIDTH], U8, "w1_sc", tag="e_scale_table")
         quantise(w1_codes[:], w1_sc[:], w1_dealt[:].rearrange("p t m j -> p (t m j)"))
-        deal(w2_dealt, w2_raw, 88)
+        deal_shared(w2_dealt, w2_raw, W2_ON_VECTOR)
 
-        def product(acc, w_codes, w_sc, t, codes, sc, b, start, stop):
-            nc.tensor.matmul_mx(
-                acc[:, t, :],
-                lhsT=w_codes[:, cols(t)].bitcast(FP8X4),
-                lhsT_scale=w_sc[:, cols(t)],
-                rhs=codes[:, cols(b)].bitcast(FP8X4),
-                rhs_scale=sc[:, cols(b)],
-                start=start,
-                stop=stop,
-            )
+        h_acc = [psum.tile([P, PACK, BLOCK], F32, name="h_acc_%d" % b) for b in range(BLOCKS)]
+        y_acc = [psum.tile([P, PACK, BLOCK], F32, name="y_acc_%d" % b) for b in range(BLOCKS)]
+        for r in range(WARM_UP_PASSES):
+            product(y_acc[r][:].rearrange("p t n -> p (t n)"), w1_codes, w1_sc, 0, x_codes[:], x_sc[:], True, True)
+        for b in range(BLOCKS):
+            product(h_acc[b][:, 0, :], w1_codes, w1_sc, 0, x_codes[:, cols(b)], x_sc[:, cols(b)], True, False)
 
         h_values = []
         for b in range(BLOCKS):
@@ -133,42 +147,45 @@ def tile_picked_zeagle_gelu_po_kernel(
             nc.vector.tensor_copy(e_codes[:, cols(b)], e_table[:].indirect(tok_sb[:, entries]))
             if b == 0:
                 quantise_slices(w2_codes, w2_sc, w2_dealt)
-            acc = psum.tile([P, PACK, BLOCK], F32, name="h_acc_%d" % b)
             for t in range(PACK):
-                product(acc, w1_codes, w1_sc, t, x_codes, x_sc, b, True, False)
-                product(acc, w2_codes, w2_sc, t, e_codes, e_sc, b, False, True)
+                acc = h_acc[b][:, t, :]
+                if t > 0:
+                    product(acc, w1_codes, w1_sc, t, x_codes[:, cols(b)], x_sc[:, cols(b)], True, False)
+                product(acc, w2_codes, w2_sc, t, e_codes[:, cols(b)], e_sc[E_SCALE_START:P, cols(b)], False, True)
             h = sbuf([P, BLOCK, PACK], BF16, "h_%d" % b)
-            nc.scalar.activation(h[:], acc[:].rearrange("p t n -> p n t"), GELU)
+            nc.scalar.activation(h[:], h_acc[b][:].rearrange("p t n -> p n t"), GELU)
             h_values.append(h)
-            if b == 1:
-                deal(w3_dealt, w3_raw, 88)
 
-        quantise(h_codes[:, cols(0)], h_sc[:, cols(0)], h_values[0][:].rearrange("p n t -> p (n t)"))
+        deal(nc.vector.tensor_copy, w3_dealt, w3_raw, slice(0, P))
+        h_codes = sbuf([P, WIDTH], U32, "h_codes", tag="w3_raw")
+        quantise_block(h_codes, h_sc, h_values[0], 0)
         quantise_slices(w3_codes, w3_sc, w3_dealt)
         for b in range(1, BLOCKS):
-            quantise(h_codes[:, cols(b)], h_sc[:, cols(b)], h_values[b][:].rearrange("p n t -> p (n t)"))
+            quantise_block(h_codes, h_sc, h_values[b], b)
 
         out_rows = out_0.rearrange("(p t) n -> p t n", t=PACK)
         out_words = out_1[0].rearrange("p n t -> p (n t)").bitcast(I32)
+        last = BLOCKS - 1
         rounded = []
         for b in range(BLOCKS):
-            acc = psum.tile([P, PACK, BLOCK], F32, name="y_acc_%d" % b)
             for t in range(PACK):
-                product(acc, w3_codes, w3_sc, t, h_codes, h_sc, b, True, True)
+                product(y_acc[b][:, t, :], w3_codes, w3_sc, t, h_codes[:, cols(b)], h_sc[:, cols(b)], True, True)
             y = sbuf([P, PACK, BLOCK], F32, "y_%d" % b)
-            nc.vector.tensor_tensor(y[:], acc[:], skip_sb[b // 2][:, :, cols(b % 2)], ADD)
+            nc.vector.tensor_tensor(y[:], y_acc[b][:], skip_sb[b // 2][:, :, cols(b % 2)], ADD)
             nc.sync.dma_start(out_rows[:, :, cols(b)], y[:])
             y16 = sbuf([P, BLOCK, PACK], BF16, "y16_%d" % b)
-            nc.scalar.copy(
-                y16[:].rearrange("p (c i) t -> p c t i", i=PACK), y[:].rearrange("p t (c i) -> p c t i", i=PACK)
-            )
+            target = y16[:].rearrange("p (c i) t -> p c t i", i=PACK)
+            source = y[:].rearrange("p t (c i) -> p c t i", i=PACK)
+            on_scalar = LAST_ON_SCALAR if b == last else BLOCK // PACK
+            nc.scalar.copy(target[:, 0:on_scalar], source[:, 0:on_scalar])
             rounded.append(y16)
             if b > 0:
-                quantise(y_codes[:, cols(b - 1)], y_sc[:, cols(b - 1)], rounded[b - 1][:].rearrange("p n t -> p (n t)"))
-        last = BLOCKS - 1
+                quantise_block(y_codes, y_sc, rounded[b - 1], b - 1)
+            if b == last:
+                nc.vector.tensor_copy(target[:, on_scalar:], source[:, on_scalar:])
         nc.sync.dma_start(out_words[:, 0 : last * BLOCK], y_codes[:, 0 : last * BLOCK].bitcast(I32))
-        quantise(y_codes[:, cols(last)], y_sc[:, cols(last)], rounded[last][:].rearrange("p n t -> p (n t)"))
+        quantise_block(y_codes, y_sc, rounded[last], last)
         nc.sync.dma_start(out_words[:, cols(last)], y_codes[:, cols(last)].bitcast(I32))
-        for q in range(4):
-            queue = nc.scalar if q % 2 == 0 else nc.sync
-            queue.dma_start(out_2[0, 4 * q : 4 * q + 4, :].bitcast(I32), y_sc[32 * q : 32 * q + 4, :].bitcast(I32))
+        for r in range(PACK):
+            queue = nc.scalar if r % 2 == 0 else nc.sync
+            queue.dma_start(out_2[0, r:SCALE_ROWS:PACK, :].bitcast(I32), y_sc[r:P:QUADRANT, :].bitcast(I32))

from contextlib import ExitStack

import concourse.mybir as mybir

F32 = mybir.dt.float32
BF16 = mybir.dt.bfloat16
I32 = mybir.dt.int32
U32 = mybir.dt.uint32
U16 = mybir.dt.uint16
U8 = mybir.dt.uint8
FP8X4 = mybir.dt.float8_e4m3fn_x4
GELU = mybir.ActivationFunctionType.Gelu_apprx_tanh
ADD = mybir.AluOpType.add

P = 128
PACK = 4
QUADRANT = 32
SCALE_ROWS = 16
WIDTH = 512
TABLE = 1024
BLOCK = 128
BLOCKS = WIDTH // BLOCK
HALF = WIDTH // 2
PER_COLUMN = 16

E_SCALE_START = 4
W1_ON_VECTOR = 32
W2_ON_VECTOR = 80
LAST_ON_SCALAR = BLOCK // PACK // 2
WARM_UP_PASSES = 2

FLOPS = 3 * 2 * WIDTH * WIDTH * WIDTH


def tile_picked_zeagle_gelu_po_kernel(
    tc, x_words, x_scales, e_words, e_scales, w1, w2, w3, skip, offs, tok, out_0, out_1, out_2
):
    nc = tc.nc
    with ExitStack() as ctx:
        keep = ctx.enter_context(tc.tile_pool(name="keep", bufs=1))
        psum = ctx.enter_context(tc.psum_pool(name="psum", bufs=1))

        def sbuf(shape, dtype, name, tag=None):
            return keep.tile(shape, dtype, name=name, tag=tag or name, align_bytes=64)

        def cols(b):
            return slice(b * BLOCK, (b + 1) * BLOCK)

        def load_words(table, words):
            nc.sync.dma_start(table[:].bitcast(I32), words[0].rearrange("p n t -> p (n t)").bitcast(I32))

        def load_scales(table, scales, start):
            for r in range(PACK):
                nc.sync.dma_start(
                    table[start + r : P : QUADRANT, :].bitcast(I32), scales[0, r:SCALE_ROWS:PACK, :].bitcast(I32)
                )

        def load_rows(matrix, name):
            rows = sbuf([P, PACK, matrix.shape[1]], F32, name)
            nc.sync.dma_start(rows[:], matrix.rearrange("(p j) c -> p j c", j=PACK))
            return rows

        def deal(copy, dealt, raw, groups):
            source = raw[:].rearrange("p j (m t) -> p m j t", t=PACK)
            target = dealt[:].rearrange("p t m j -> p m j t")
            copy(target[:, groups], source[:, groups])

        def deal_shared(dealt, raw, on_vector):
            deal(nc.scalar.copy, dealt, raw, slice(on_vector, P))
            deal(nc.vector.tensor_copy, dealt, raw, slice(0, on_vector))

        def quantise(codes, scales, values):
            nc.vector.quantize_mx(codes.bitcast(FP8X4), scales, values)

        def quantise_slices(codes, scales, dealt):
            for t in range(PACK):
                quantise(codes[:, cols(t)], scales[:, cols(t)], dealt[:, t].rearrange("p m j -> p (m j)"))

        def quantise_block(codes, scales, values, b):
            quantise(codes[:, cols(b)], scales[:, cols(b)], values[:].rearrange("p n t -> p (n t)"))

        def product(acc, w_codes, w_scales, t, codes, scales, start, stop):
            nc.tensor.matmul_mx(
                acc,
                lhsT=w_codes[:, cols(t)].bitcast(FP8X4),
                lhsT_scale=w_scales[:, cols(t)],
                rhs=codes.bitcast(FP8X4),
                rhs_scale=scales,
                start=start,
                stop=stop,
            )

        offs_sb = keep.tile([P, WIDTH // PER_COLUMN], U16, name="offs_sb")
        tok_sb = keep.tile([P, WIDTH // PER_COLUMN], U16, name="tok_sb")
        x_table = sbuf([P, TABLE], U32, "x_table")
        e_table = sbuf([P, TABLE], U32, "e_table")
        x_scale_table = sbuf([P, TABLE], U8, "x_scale_table")
        e_scale_table = sbuf([P, TABLE], U8, "e_scale_table")

        warm_in = sbuf([P, 1], F32, "warm_in")
        warm_out = sbuf([P, 1], F32, "warm_out")
        nc.vector.memset(x_scale_table[:].bitcast(I32), 0)
        nc.gpsimd.memset(e_scale_table[:].bitcast(I32), 0)
        nc.vector.memset(warm_in[:], 0.0)
        nc.scalar.activation(warm_out[:], warm_in[:], GELU)

        load_words(x_table, x_words)
        nc.sync.dma_start(offs_sb[:], offs)
        nc.sync.dma_start(tok_sb[:], tok)
        load_scales(x_scale_table, x_scales, 0)
        w1_raw = load_rows(w1, "w1_raw")
        load_scales(e_scale_table, e_scales, E_SCALE_START)
        w2_raw = load_rows(w2, "w2_raw")
        load_words(e_table, e_words)
        w3_raw = load_rows(w3, "w3_raw")
        skip_sb = [load_rows(skip[:, u * HALF : (u + 1) * HALF], "skip_%d" % u) for u in range(2)]

        x_codes, x_sc = sbuf([P, WIDTH], U32, "x_codes"), sbuf([P, WIDTH], U8, "x_sc")
        e_codes, e_sc = sbuf([P, WIDTH], U32, "e_codes"), sbuf([P, WIDTH], U8, "e_sc")
        w1_codes = sbuf([P, WIDTH], U32, "w1_codes")
        w2_codes, w2_sc = sbuf([P, WIDTH], U32, "w2_codes"), sbuf([P, WIDTH], U8, "w2_sc")
        w3_codes, w3_sc = sbuf([P, WIDTH], U32, "w3_codes"), sbuf([P, WIDTH], U8, "w3_sc")
        h_sc = sbuf([P, WIDTH], U8, "h_sc")
        y_codes, y_sc = sbuf([P, WIDTH], U32, "y_codes"), sbuf([P, WIDTH], U8, "y_sc")
        w1_dealt = sbuf([P, PACK, P, PACK], BF16, "w1_dealt")
        w2_dealt = sbuf([P, PACK, P, PACK], BF16, "w2_dealt")
        w3_dealt = sbuf([P, PACK, P, PACK], BF16, "w3_dealt")

        nc.vector.tensor_copy(x_codes[:], x_table[:].indirect(offs_sb[:]))
        nc.vector.tensor_copy(x_sc[:], x_scale_table[:].indirect(offs_sb[:]))
        nc.vector.tensor_copy(e_sc[:], e_scale_table[:].indirect(tok_sb[:]))
        deal_shared(w1_dealt, w1_raw, W1_ON_VECTOR)
        w1_sc = sbuf([P, WIDTH], U8, "w1_sc", tag="e_scale_table")
        quantise(w1_codes[:], w1_sc[:], w1_dealt[:].rearrange("p t m j -> p (t m j)"))
        deal_shared(w2_dealt, w2_raw, W2_ON_VECTOR)

        h_acc = [psum.tile([P, PACK, BLOCK], F32, name="h_acc_%d" % b) for b in range(BLOCKS)]
        y_acc = [psum.tile([P, PACK, BLOCK], F32, name="y_acc_%d" % b) for b in range(BLOCKS)]
        for r in range(WARM_UP_PASSES):
            product(y_acc[r][:].rearrange("p t n -> p (t n)"), w1_codes, w1_sc, 0, x_codes[:], x_sc[:], True, True)
        for b in range(BLOCKS):
            product(h_acc[b][:, 0, :], w1_codes, w1_sc, 0, x_codes[:, cols(b)], x_sc[:, cols(b)], True, False)

        h_values = []
        for b in range(BLOCKS):
            entries = slice(b * BLOCK // PER_COLUMN, (b + 1) * BLOCK // PER_COLUMN)
            nc.vector.tensor_copy(e_codes[:, cols(b)], e_table[:].indirect(tok_sb[:, entries]))
            if b == 0:
                quantise_slices(w2_codes, w2_sc, w2_dealt)
            for t in range(PACK):
                acc = h_acc[b][:, t, :]
                if t > 0:
                    product(acc, w1_codes, w1_sc, t, x_codes[:, cols(b)], x_sc[:, cols(b)], True, False)
                product(acc, w2_codes, w2_sc, t, e_codes[:, cols(b)], e_sc[E_SCALE_START:P, cols(b)], False, True)
            h = sbuf([P, BLOCK, PACK], BF16, "h_%d" % b)
            nc.scalar.activation(h[:], h_acc[b][:].rearrange("p t n -> p n t"), GELU)
            h_values.append(h)

        deal(nc.vector.tensor_copy, w3_dealt, w3_raw, slice(0, P))
        h_codes = sbuf([P, WIDTH], U32, "h_codes", tag="w3_raw")
        quantise_block(h_codes, h_sc, h_values[0], 0)
        quantise_slices(w3_codes, w3_sc, w3_dealt)
        for b in range(1, BLOCKS):
            quantise_block(h_codes, h_sc, h_values[b], b)

        out_rows = out_0.rearrange("(p t) n -> p t n", t=PACK)
        out_words = out_1[0].rearrange("p n t -> p (n t)").bitcast(I32)
        last = BLOCKS - 1
        rounded = []
        for b in range(BLOCKS):
            for t in range(PACK):
                product(y_acc[b][:, t, :], w3_codes, w3_sc, t, h_codes[:, cols(b)], h_sc[:, cols(b)], True, True)
            y = sbuf([P, PACK, BLOCK], F32, "y_%d" % b)
            nc.vector.tensor_tensor(y[:], y_acc[b][:], skip_sb[b // 2][:, :, cols(b % 2)], ADD)
            nc.sync.dma_start(out_rows[:, :, cols(b)], y[:])
            y16 = sbuf([P, BLOCK, PACK], BF16, "y16_%d" % b)
            target = y16[:].rearrange("p (c i) t -> p c t i", i=PACK)
            source = y[:].rearrange("p t (c i) -> p c t i", i=PACK)
            on_scalar = LAST_ON_SCALAR if b == last else BLOCK // PACK
            nc.scalar.copy(target[:, 0:on_scalar], source[:, 0:on_scalar])
            rounded.append(y16)
            if b > 0:
                quantise_block(y_codes, y_sc, rounded[b - 1], b - 1)
            if b == last:
                nc.vector.tensor_copy(target[:, on_scalar:], source[:, on_scalar:])
        nc.sync.dma_start(out_words[:, 0 : last * BLOCK], y_codes[:, 0 : last * BLOCK].bitcast(I32))
        quantise_block(y_codes, y_sc, rounded[last], last)
        nc.sync.dma_start(out_words[:, cols(last)], y_codes[:, cols(last)].bitcast(I32))
        for r in range(PACK):
            queue = nc.scalar if r % 2 == 0 else nc.sync
            queue.dma_start(out_2[0, r:SCALE_ROWS:PACK, :].bitcast(I32), y_sc[r:P:QUADRANT, :].bitcast(I32))
